import numpy as np, ml_dtypes
CORES = [3,7,11,15,19,23,27,31,35,39,43,47,51,55,59,63]
N = 16
ROOT = 0
def setup_inputs(rng):
    return {"x": rng.standard_normal((N, 128, N * 1024), dtype=np.float32).astype(ml_dtypes.bfloat16)}
def reference(x):
    return {"y": np.stack([x[ROOT][:, r * 1024:(r + 1) * 1024] for r in range(N)])}

@@ -1,0 +1,69 @@
+from concourse.bass import RemoteDMATransfer, DstId
+W = 1024
+ROOT = 3
+SCRATCH = {'stage': ('sbuf', [128, 16 * W], 'bfloat16')}
+SEMAPHORES = ['ld%d' % i for i in range(8)] + ['p%d' % i for i in range(32)] + ['sent', 'stored']
+LOOKAHEAD = 2
+
+def blk(b):
+    return (b * W, (b + 1) * W)
+STEPS = [([(12 * W, 16 * W)], [(15, blk(15), [6, 63], 3840), (13, blk(13), [4, 55], 61440), (14, blk(14), [2, 59], 15), (12, blk(12), [0, 51], 240)]), ([(8 * W, 12 * W)], [(11, blk(11), [7, 47], 3840), (9, blk(9), [5, 39], 61440), (10, blk(10), [2, 43], 15), (8, blk(8), [1, 35], 240)]), ([(4 * W, 8 * W)], [(7, blk(7), [6, 31], 3840), (5, blk(5), [4, 23], 61440), (6, blk(6), [2, 27], 15), (4, blk(4), [0, 19], 240)]), ([(1 * W, 4 * W)], [(3, blk(3), [7, 15], 65280), (2, blk(2), [11], 15), (1, blk(1), [7], 240)])]
+
+def popcount(m):
+    return bin(m).count('1')
+
+def rank_program(g, core, T, topo):
+    s = T.sem
+    LD = [s.ld0, s.ld1, s.ld2, s.ld3, s.ld4, s.ld5, s.ld6, s.ld7]
+    P = [s.p0, s.p1, s.p2, s.p3, s.p4, s.p5, s.p6, s.p7, s.p8, s.p9, s.p10, s.p11, s.p12, s.p13, s.p14, s.p15, s.p16, s.p17, s.p18, s.p19, s.p20, s.p21, s.p22, s.p23, s.p24, s.p25, s.p26, s.p27, s.p28, s.p29, s.p30, s.p31]
+    stage = T.stage
+    if core == ROOT:
+        n = len(STEPS)
+
+        def load(k):
+            for a, b in STEPS[k][0]:
+                g.dma_start(stage[:, a:b], T.x[:, a:b]).then_inc(LD[k], 16)
+        for k in range(min(LOOKAHEAD, n)):
+            load(k)
+        sent = 0
+        for k in range(n):
+            loads, sends = STEPS[k]
+            g.wait_ge(LD[k], 16 * len(loads))
+            trs = []
+            for pid_, (a, b), route, mask in sends:
+                rid, pnc, se = topo.addr(route[0])
+                trs.append(RemoteDMATransfer(dst_ids=[DstId(rid=rid, pnc=pnc)], dma_engine_mask=mask, remote_sem=P[pid_], src=stage[:, a:b], dst=stage[:, a:b]))
+                sent += popcount(mask)
+            g.remote_dma_fused(trs, local_sem=s.sent)
+            if k + LOOKAHEAD < n:
+                load(k + LOOKAHEAD)
+        g.dma_start(T.y[:, :], T.x[:, 0:W]).then_inc(s.stored, 16)
+        g.wait_ge(s.sent, sent)
+        g.wait_ge(s.stored, 16)
+        return
+    rank = T.rank_of(core)
+    sent = 0
+    stored = 0
+    for loads, sends in STEPS:
+        for pid_, (a, b), route, mask in sends:
+            if core not in route:
+                continue
+            h = route.index(core)
+            if h == 0:
+                inc = popcount(mask)
+            else:
+                inc = popcount(topo.mask(route[h - 1], core))
+            g.wait_ge(P[pid_], inc)
+            if h + 1 < len(route):
+                nxt = route[h + 1]
+                rid, pnc, se = topo.addr(nxt)
+                m = topo.mask(core, nxt)
+                g.remote_dma(stage[:, a:b], stage[:, a:b], P[pid_], s.sent, pnc, rid, m)
+                sent += popcount(m)
+            else:
+                g.dma_start(T.y[:, a - rank * W:b - rank * W], stage[:, a:b]).then_inc(s.stored, 16)
+                stored += 16
+    if sent:
+        g.wait_ge(s.sent, sent)
+    if stored:
+        g.wait_ge(s.stored, stored)

@@ -5,12 +5,20 @@ SCRATCH = {'stage': ('sbuf', [128, 16 * W], 'bfloat16')}
 SEMAPHORES = ['ld%d' % i for i in range(8)] + ['p%d' % i for i in range(32)] + ['sent', 'stored']
 LOOKAHEAD = 2
 
+
 def blk(b):
     return (b * W, (b + 1) * W)
-STEPS = [([(12 * W, 16 * W)], [(15, blk(15), [6, 63], 3840), (13, blk(13), [4, 55], 61440), (14, blk(14), [2, 59], 15), (12, blk(12), [0, 51], 240)]), ([(8 * W, 12 * W)], [(11, blk(11), [7, 47], 3840), (9, blk(9), [5, 39], 61440), (10, blk(10), [2, 43], 15), (8, blk(8), [1, 35], 240)]), ([(4 * W, 8 * W)], [(7, blk(7), [6, 31], 3840), (5, blk(5), [4, 23], 61440), (6, blk(6), [2, 27], 15), (4, blk(4), [0, 19], 240)]), ([(1 * W, 4 * W)], [(3, blk(3), [7, 15], 65280), (2, blk(2), [11], 15), (1, blk(1), [7], 240)])]
+
+
+STEPS = [((12 * W, 16 * W), [(15, blk(15), [6, 63], 3840), (13, blk(13), [4, 55], 61440), (14, blk(14), [2, 59], 15), (12, blk(12), [0, 51], 240)]),
+         ((8 * W, 12 * W), [(11, blk(11), [7, 47], 3840), (9, blk(9), [5, 39], 61440), (10, blk(10), [2, 43], 15), (8, blk(8), [1, 35], 240)]),
+         ((4 * W, 8 * W), [(7, blk(7), [6, 31], 3840), (5, blk(5), [4, 23], 61440), (6, blk(6), [2, 27], 15), (4, blk(4), [0, 19], 240)]),
+         ((1 * W, 4 * W), [(3, blk(3), [7, 15], 65280), (2, blk(2), [11], 15), (1, blk(1), [7], 240)])]
+
 
 def popcount(m):
     return bin(m).count('1')
+
 
 def rank_program(g, core, T, topo):
     s = T.sem
@@ -19,32 +27,31 @@ def rank_program(g, core, T, topo):
     stage = T.stage
     if core == ROOT:
         n = len(STEPS)
-
-        def load(k):
-            for a, b in STEPS[k][0]:
-                g.dma_start(stage[:, a:b], T.x[:, a:b]).then_inc(LD[k], 16)
-        for k in range(min(LOOKAHEAD, n)):
-            load(k)
+        qs = [g.sync, g.scalar]
+        for k in range(n):
+            q = qs[k % 2]
+            if k >= LOOKAHEAD:
+                q.wait_ge(LD[k - LOOKAHEAD], 16)
+            a, b = STEPS[k][0]
+            q.dma_start(stage[:, a:b], T.x[:, a:b]).then_inc(LD[k], 16)
+        qs[n % 2].dma_start(T.y[:, :], T.x[:, 0:W]).then_inc(s.stored, 16)
         sent = 0
         for k in range(n):
-            loads, sends = STEPS[k]
-            g.wait_ge(LD[k], 16 * len(loads))
+            _, sends = STEPS[k]
+            g.wait_ge(LD[k], 16)
             trs = []
             for pid_, (a, b), route, mask in sends:
                 rid, pnc, se = topo.addr(route[0])
                 trs.append(RemoteDMATransfer(dst_ids=[DstId(rid=rid, pnc=pnc)], dma_engine_mask=mask, remote_sem=P[pid_], src=stage[:, a:b], dst=stage[:, a:b]))
                 sent += popcount(mask)
             g.remote_dma_fused(trs, local_sem=s.sent)
-            if k + LOOKAHEAD < n:
-                load(k + LOOKAHEAD)
-        g.dma_start(T.y[:, :], T.x[:, 0:W]).then_inc(s.stored, 16)
         g.wait_ge(s.sent, sent)
         g.wait_ge(s.stored, 16)
         return
     rank = T.rank_of(core)
     sent = 0
     stored = 0
-    for loads, sends in STEPS:
+    for _, sends in STEPS:
         for pid_, (a, b), route, mask in sends:
             if core not in route:
                 continue
@@ -53,15 +60,16 @@ def rank_program(g, core, T, topo):
                 inc = popcount(mask)
             else:
                 inc = popcount(topo.mask(route[h - 1], core))
-            g.wait_ge(P[pid_], inc)
             if h + 1 < len(route):
+                g.wait_ge(P[pid_], inc)
                 nxt = route[h + 1]
                 rid, pnc, se = topo.addr(nxt)
                 m = topo.mask(core, nxt)
                 g.remote_dma(stage[:, a:b], stage[:, a:b], P[pid_], s.sent, pnc, rid, m)
                 sent += popcount(m)
             else:
-                g.dma_start(T.y[:, a - rank * W:b - rank * W], stage[:, a:b]).then_inc(s.stored, 16)
+                g.sync.wait_ge(P[pid_], inc)
+                g.sync.dma_start(T.y[:, a - rank * W:b - rank * W], stage[:, a:b]).then_inc(s.stored, 16)
                 stored += 16
     if sent:
         g.wait_ge(s.sent, sent)

@@ -4,20 +4,40 @@ ROOT = 3
 SCRATCH = {'stage': ('sbuf', [128, 16 * W], 'bfloat16')}
 SEMAPHORES = ['ld%d' % i for i in range(8)] + ['p%d' % i for i in range(32)] + ['sent', 'stored']
 LOOKAHEAD = 2
+CORES = [3 + 4 * i for i in range(16)]
+
+Q0, Q1, Q2, Q3, E07, E8F = 0x000F, 0x00F0, 0x0F00, 0xF000, 0x00FF, 0xFF00
 
 
-def blk(b):
-    return (b * W, (b + 1) * W)
+def fin(r, mask):
+    return (r, r * W, (r + 1) * W, CORES[r], mask)
 
 
-STEPS = [((12 * W, 16 * W), [(15, blk(15), [6, 63], 3840), (13, blk(13), [4, 55], 61440), (14, blk(14), [2, 59], 15), (12, blk(12), [0, 51], 240)]),
-         ((8 * W, 12 * W), [(11, blk(11), [7, 47], 3840), (9, blk(9), [5, 39], 61440), (10, blk(10), [2, 43], 15), (8, blk(8), [1, 35], 240)]),
-         ((4 * W, 8 * W), [(7, blk(7), [6, 31], 3840), (5, blk(5), [4, 23], 61440), (6, blk(6), [2, 27], 15), (4, blk(4), [0, 19], 240)]),
-         ((1 * W, 4 * W), [(3, blk(3), [7, 15], 65280), (2, blk(2), [11], 15), (1, blk(1), [7], 240)])]
+def via(r, helper, mask):
+    return (16 + r, r * W, (r + 1) * W, helper, mask)
+
+
+STEPS = [((11 * W, 16 * W), [via(14, 2, Q0), via(11, 7, Q1), via(15, 6, Q2), via(13, 4, Q3)]),
+         ((7 * W, 11 * W), [via(10, 2, Q0), via(12, 0, Q1), via(7, 6, Q2), via(9, 5, Q3)]),
+         ((3 * W, 7 * W), [fin(6, Q0), fin(8, Q1), via(3, 7, Q2), via(5, 4, Q3)]),
+         ((1 * W, 3 * W), [fin(2, Q0), fin(4, Q1), fin(1, E8F)])]
+RELAY = {}
+for _, call in STEPS:
+    for t in call:
+        if t[0] >= 16:
+            RELAY.setdefault(t[3], []).append(t[0] - 16)
 
 
 def popcount(m):
     return bin(m).count('1')
+
+
+INC = {}
+for _, call in STEPS:
+    for t in call:
+        INC[t[0]] = popcount(t[4])
+        if t[0] >= 16:
+            INC[t[0] - 16] = 8
 
 
 def rank_program(g, core, T, topo):
@@ -25,6 +45,17 @@ def rank_program(g, core, T, topo):
     LD = [s.ld0, s.ld1, s.ld2, s.ld3, s.ld4, s.ld5, s.ld6, s.ld7]
     P = [s.p0, s.p1, s.p2, s.p3, s.p4, s.p5, s.p6, s.p7, s.p8, s.p9, s.p10, s.p11, s.p12, s.p13, s.p14, s.p15, s.p16, s.p17, s.p18, s.p19, s.p20, s.p21, s.p22, s.p23, s.p24, s.p25, s.p26, s.p27, s.p28, s.p29, s.p30, s.p31]
     stage = T.stage
+
+    def fused(call):
+        trs = []
+        n = 0
+        for sem, a, b, dst, mask in call:
+            rid, pnc, se = topo.addr(dst)
+            trs.append(RemoteDMATransfer(dst_ids=[DstId(rid=rid, pnc=pnc)], dma_engine_mask=mask, remote_sem=P[sem], src=stage[:, a:b], dst=stage[:, a:b]))
+            n += popcount(mask)
+        g.remote_dma_fused(trs, local_sem=s.sent)
+        return n
+
     if core == ROOT:
         n = len(STEPS)
         qs = [g.sync, g.scalar]
@@ -34,44 +65,23 @@ def rank_program(g, core, T, topo):
                 q.wait_ge(LD[k - LOOKAHEAD], 16)
             a, b = STEPS[k][0]
             q.dma_start(stage[:, a:b], T.x[:, a:b]).then_inc(LD[k], 16)
-        qs[n % 2].dma_start(T.y[:, :], T.x[:, 0:W]).then_inc(s.stored, 16)
         sent = 0
         for k in range(n):
-            _, sends = STEPS[k]
             g.wait_ge(LD[k], 16)
-            trs = []
-            for pid_, (a, b), route, mask in sends:
-                rid, pnc, se = topo.addr(route[0])
-                trs.append(RemoteDMATransfer(dst_ids=[DstId(rid=rid, pnc=pnc)], dma_engine_mask=mask, remote_sem=P[pid_], src=stage[:, a:b], dst=stage[:, a:b]))
-                sent += popcount(mask)
-            g.remote_dma_fused(trs, local_sem=s.sent)
+            sent += fused(STEPS[k][1])
+        g.dma_start(T.y[:, :], T.x[:, 0:W]).then_inc(s.stored, 16)
         g.wait_ge(s.sent, sent)
         g.wait_ge(s.stored, 16)
         return
-    rank = T.rank_of(core)
+    rank = T.rank_of(core) if core in CORES else None
+    if rank is not None:
+        g.sync.wait_ge(P[rank], INC[rank])
+        g.sync.dma_start(T.y[:, :], stage[:, rank * W:(rank + 1) * W]).then_inc(s.stored, 16)
     sent = 0
-    stored = 0
-    for _, sends in STEPS:
-        for pid_, (a, b), route, mask in sends:
-            if core not in route:
-                continue
-            h = route.index(core)
-            if h == 0:
-                inc = popcount(mask)
-            else:
-                inc = popcount(topo.mask(route[h - 1], core))
-            if h + 1 < len(route):
-                g.wait_ge(P[pid_], inc)
-                nxt = route[h + 1]
-                rid, pnc, se = topo.addr(nxt)
-                m = topo.mask(core, nxt)
-                g.remote_dma(stage[:, a:b], stage[:, a:b], P[pid_], s.sent, pnc, rid, m)
-                sent += popcount(m)
-            else:
-                g.sync.wait_ge(P[pid_], inc)
-                g.sync.dma_start(T.y[:, a - rank * W:b - rank * W], stage[:, a:b]).then_inc(s.stored, 16)
-                stored += 16
+    for r in RELAY.get(core, []):
+        g.wait_ge(P[16 + r], INC[16 + r])
+        sent += fused([fin(r, E07)])
     if sent:
         g.wait_ge(s.sent, sent)
-    if stored:
-        g.wait_ge(s.stored, stored)
+    if rank is not None:
+        g.wait_ge(s.stored, 16)

@@ -6,7 +6,7 @@ SEMAPHORES = ['ld%d' % i for i in range(8)] + ['p%d' % i for i in range(32)] + [
 LOOKAHEAD = 2
 CORES = [3 + 4 * i for i in range(16)]
 
-Q0, Q1, Q2, Q3, E07, E8F = 0x000F, 0x00F0, 0x0F00, 0xF000, 0x00FF, 0xFF00
+Q0, Q1, Q2, Q3, E07, E8F, ALL = 0x000F, 0x00F0, 0x0F00, 0xF000, 0x00FF, 0xFF00, 0xFFFF
 
 
 def fin(r, mask):
@@ -17,27 +17,25 @@ def via(r, helper, mask):
     return (16 + r, r * W, (r + 1) * W, helper, mask)
 
 
-STEPS = [((11 * W, 16 * W), [via(14, 2, Q0), via(11, 7, Q1), via(15, 6, Q2), via(13, 4, Q3)]),
-         ((7 * W, 11 * W), [via(10, 2, Q0), via(12, 0, Q1), via(7, 6, Q2), via(9, 5, Q3)]),
-         ((3 * W, 7 * W), [fin(6, Q0), fin(8, Q1), via(3, 7, Q2), via(5, 4, Q3)]),
-         ((1 * W, 3 * W), [fin(2, Q0), fin(4, Q1), fin(1, E8F)])]
-RELAY = {}
-for _, call in STEPS:
-    for t in call:
-        if t[0] >= 16:
-            RELAY.setdefault(t[3], []).append(t[0] - 16)
+STEPS = [((11 * W, 16 * W), [[via(14, 2, Q0), via(11, 7, Q1), via(15, 6, Q2), via(13, 4, Q3)], [via(12, 0, ALL)]]),
+         ((7 * W, 11 * W), [[via(10, 2, E07), via(7, 6, Q2), via(9, 5, Q3)]]),
+         ((3 * W, 7 * W), [[fin(6, Q0), fin(8, Q1), via(3, 7, Q2), via(5, 4, Q3)]]),
+         ((1 * W, 3 * W), [[fin(2, Q0), fin(4, Q1), fin(1, E8F)]])]
 
 
 def popcount(m):
     return bin(m).count('1')
 
 
+RELAY = {}
 INC = {}
-for _, call in STEPS:
-    for t in call:
-        INC[t[0]] = popcount(t[4])
-        if t[0] >= 16:
-            INC[t[0] - 16] = 8
+for _, calls in STEPS:
+    for call in calls:
+        for t in call:
+            INC[t[0]] = popcount(t[4])
+            if t[0] >= 16:
+                INC[t[0] - 16] = 8
+                RELAY.setdefault(t[3], []).append(t[0] - 16)
 
 
 def rank_program(g, core, T, topo):
@@ -68,7 +66,8 @@ def rank_program(g, core, T, topo):
         sent = 0
         for k in range(n):
             g.wait_ge(LD[k], 16)
-            sent += fused(STEPS[k][1])
+            for call in STEPS[k][1]:
+                sent += fused(call)
         g.dma_start(T.y[:, :], T.x[:, 0:W]).then_inc(s.stored, 16)
         g.wait_ge(s.sent, sent)
         g.wait_ge(s.stored, 16)

@@ -17,8 +17,10 @@ def via(r, helper, mask):
     return (16 + r, r * W, (r + 1) * W, helper, mask)
 
 
-STEPS = [((11 * W, 16 * W), [[via(14, 2, Q0), via(11, 7, Q1), via(15, 6, Q2), via(13, 4, Q3)], [via(12, 0, ALL)]]),
-         ((7 * W, 11 * W), [[via(10, 2, E07), via(7, 6, Q2), via(9, 5, Q3)]]),
+STEPS = [((14 * W, 16 * W), [[via(14, 2, E07), via(15, 6, E8F)]]),
+         ((12 * W, 14 * W), [[via(12, 0, E07), via(13, 4, E8F)]]),
+         ((10 * W, 12 * W), [[via(10, 2, E07), via(11, 7, E8F)]]),
+         ((7 * W, 10 * W), [[via(7, 6, ALL)], [via(9, 5, E8F)]]),
          ((3 * W, 7 * W), [[fin(6, Q0), fin(8, Q1), via(3, 7, Q2), via(5, 4, Q3)]]),
          ((1 * W, 3 * W), [[fin(2, Q0), fin(4, Q1), fin(1, E8F)]])]
 

@@ -2,7 +2,7 @@ from concourse.bass import RemoteDMATransfer, DstId
 W = 1024
 ROOT = 3
 SCRATCH = {'stage': ('sbuf', [128, 16 * W], 'bfloat16')}
-SEMAPHORES = ['ld%d' % i for i in range(8)] + ['p%d' % i for i in range(32)] + ['sent', 'stored']
+SEMAPHORES = ['ld%d' % i for i in range(8)] + ['p%d' % i for i in range(32)] + ['sent', 'stored', 'tok']
 LOOKAHEAD = 2
 CORES = [3 + 4 * i for i in range(16)]
 
@@ -62,7 +62,7 @@ def rank_program(g, core, T, topo):
         for k in range(n):
             q = qs[k % 2]
             if k >= LOOKAHEAD:
-                q.wait_ge(LD[k - LOOKAHEAD], 16)
+                q.wait_ge(s.tok, k - LOOKAHEAD + 1)
             a, b = STEPS[k][0]
             q.dma_start(stage[:, a:b], T.x[:, a:b]).then_inc(LD[k], 16)
         sent = 0
@@ -70,6 +70,8 @@ def rank_program(g, core, T, topo):
             g.wait_ge(LD[k], 16)
             for call in STEPS[k][1]:
                 sent += fused(call)
+            if k + LOOKAHEAD < n:
+                g.sem_inc(s.tok, 1)
         g.dma_start(T.y[:, :], T.x[:, 0:W]).then_inc(s.stored, 16)
         g.wait_ge(s.sent, sent)
         g.wait_ge(s.stored, 16)

from concourse.bass import RemoteDMATransfer, DstId
W = 1024
ROOT = 3
SCRATCH = {'stage': ('sbuf', [128, 16 * W], 'bfloat16')}
SEMAPHORES = ['ld%d' % i for i in range(8)] + ['p%d' % i for i in range(32)] + ['sent', 'stored', 'tok']
LOOKAHEAD = 2
CORES = [3 + 4 * i for i in range(16)]

Q0, Q1, Q2, Q3, E07, E8F, ALL = 0x000F, 0x00F0, 0x0F00, 0xF000, 0x00FF, 0xFF00, 0xFFFF


def fin(r, mask):
    return (r, r * W, (r + 1) * W, CORES[r], mask)


def via(r, helper, mask):
    return (16 + r, r * W, (r + 1) * W, helper, mask)


STEPS = [((14 * W, 16 * W), [[via(14, 2, E07), via(15, 6, E8F)]]),
         ((12 * W, 14 * W), [[via(12, 0, E07), via(13, 4, E8F)]]),
         ((10 * W, 12 * W), [[via(10, 2, E07), via(11, 7, E8F)]]),
         ((7 * W, 10 * W), [[via(7, 6, ALL)], [via(9, 5, E8F)]]),
         ((3 * W, 7 * W), [[fin(6, Q0), fin(8, Q1), via(3, 7, Q2), via(5, 4, Q3)]]),
         ((1 * W, 3 * W), [[fin(2, Q0), fin(4, Q1), fin(1, E8F)]])]


def popcount(m):
    return bin(m).count('1')


RELAY = {}
INC = {}
for _, calls in STEPS:
    for call in calls:
        for t in call:
            INC[t[0]] = popcount(t[4])
            if t[0] >= 16:
                INC[t[0] - 16] = 8
                RELAY.setdefault(t[3], []).append(t[0] - 16)


def rank_program(g, core, T, topo):
    s = T.sem
    LD = [s.ld0, s.ld1, s.ld2, s.ld3, s.ld4, s.ld5, s.ld6, s.ld7]
    P = [s.p0, s.p1, s.p2, s.p3, s.p4, s.p5, s.p6, s.p7, s.p8, s.p9, s.p10, s.p11, s.p12, s.p13, s.p14, s.p15, s.p16, s.p17, s.p18, s.p19, s.p20, s.p21, s.p22, s.p23, s.p24, s.p25, s.p26, s.p27, s.p28, s.p29, s.p30, s.p31]
    stage = T.stage

    def fused(call):
        trs = []
        n = 0
        for sem, a, b, dst, mask in call:
            rid, pnc, se = topo.addr(dst)
            trs.append(RemoteDMATransfer(dst_ids=[DstId(rid=rid, pnc=pnc)], dma_engine_mask=mask, remote_sem=P[sem], src=stage[:, a:b], dst=stage[:, a:b]))
            n += popcount(mask)
        g.remote_dma_fused(trs, local_sem=s.sent)
        return n

    if core == ROOT:
        n = len(STEPS)
        qs = [g.sync, g.scalar]
        for k in range(n):
            q = qs[k % 2]
            if k >= LOOKAHEAD:
                q.wait_ge(s.tok, k - LOOKAHEAD + 1)
            a, b = STEPS[k][0]
            q.dma_start(stage[:, a:b], T.x[:, a:b]).then_inc(LD[k], 16)
        sent = 0
        for k in range(n):
            g.wait_ge(LD[k], 16)
            for call in STEPS[k][1]:
                sent += fused(call)
            if k + LOOKAHEAD < n:
                g.sem_inc(s.tok, 1)
        g.dma_start(T.y[:, :], T.x[:, 0:W]).then_inc(s.stored, 16)
        g.wait_ge(s.sent, sent)
        g.wait_ge(s.stored, 16)
        return
    rank = T.rank_of(core) if core in CORES else None
    if rank is not None:
        g.sync.wait_ge(P[rank], INC[rank])
        g.sync.dma_start(T.y[:, :], stage[:, rank * W:(rank + 1) * W]).then_inc(s.stored, 16)
    sent = 0
    for r in RELAY.get(core, []):
        g.wait_ge(P[16 + r], INC[16 + r])
        sent += fused([fin(r, E07)])
    if sent:
        g.wait_ge(s.sent, sent)
    if rank is not None:
        g.wait_ge(s.stored, 16)
